import numpy as np
import ml_dtypes


def mxq(x, axis, fmt="e4m3"):
    dtype, down = {"e4m3": (ml_dtypes.float8_e4m3fn, 7), "e5m2": (ml_dtypes.float8_e5m2, 14)}[fmt]
    v = np.moveaxis(np.asarray(x, np.float32).astype(ml_dtypes.bfloat16).astype(np.float64), axis, -1)
    blocks = v.reshape(v.shape[:-1] + (-1, 32))
    amax = np.abs(blocks).max(-1, keepdims=True)
    byte = np.maximum(np.where(amax > 0, np.frexp(amax)[1] - 1 + 127, 0) - down, 1)
    scale = np.exp2(byte - 127.0)
    codes = (blocks / scale).astype(np.float32).astype(dtype).astype(np.float64)
    return np.moveaxis((codes * scale).reshape(v.shape), -1, axis)


WIDE = False


def mx_kscale(k):
    if not WIDE:
        return np.ones(k)
    levels = np.array([10, -10, 5, -5, 0])
    if k % 512:
        return np.exp2(np.random.permutation(np.resize(levels, k // 32))).repeat(32)
    a = np.empty((k // 512, 16))
    for p in range(k // 512):
        a[p, :8] = np.random.permutation(np.resize(levels, 8))
        for g in range(8):
            far = levels[np.abs(levels - a[p, g]) >= 10]
            a[p, g + 8] = far[np.random.randint(len(far))]
    return np.exp2(a.ravel()).repeat(32)


BF16 = ml_dtypes.bfloat16


def bf(x):
    return np.asarray(x, np.float32).astype(BF16)


def f64(x):
    return np.asarray(x).astype(np.float64)

def planes(Y):
    n, m = Y.shape
    b = f64(bf(Y)).reshape(n // 32, 32, m)
    amax = np.abs(b).max(1)
    byte = np.clip(np.where(amax > 0, np.frexp(amax)[1] - 1 + 127 - 7, 1), 1, 254)
    codes = (b * np.exp2(127.0 - byte)[:, None, :]).reshape(n, m).astype(np.float32).astype(ml_dtypes.float8_e4m3fn).view(np.uint8)
    words = codes.reshape(n // 512, 128, 4, m).transpose(0, 1, 3, 2)
    return np.ascontiguousarray(words), np.ascontiguousarray(byte.astype(np.uint8).reshape(n // 512, 16, m))


B, N, D = 1, 1024, 512


def channel_logits(q, k, tau):
    n_tokens = q.shape[1]
    s = mxq(q, 1, "e4m3").transpose(0, 2, 1) @ mxq(k, 1, "e4m3")
    return s * tau[None, :, None] / np.sqrt(n_tokens)


def softmax(l):
    e = np.exp(l - l.max(-1, keepdims=True))
    return e / e.sum(-1, keepdims=True)


def setup_inputs():
    s, t = mx_kscale(N), mx_kscale(D)
    return {"q": bf(np.random.standard_normal((B, N, D)) * s[None, :, None]),
            "k": bf(np.random.standard_normal((B, N, D)) / s[None, :, None]),
            "v": bf(np.random.standard_normal((B, N, D)) / t[None, None, :]),
            "tau": bf(np.random.uniform(1.5, 2.5, D)),
            "gain": bf((1.0 + 0.1 * np.random.standard_normal(D)) * t)}


def core(q, k, v, tau, gain):
    q, k, v, tau, gain = f64(q), f64(k), f64(v), f64(tau), f64(gain)
    d = q.shape[-1]
    l = channel_logits(q, k, tau)
    a = softmax(l)
    c = (a - 1.0 / d) * gain[None, None, :]
    return mxq(v, 2, "e4m3") @ mxq(c, 2, "e4m3").transpose(0, 2, 1)


def reference(q, k, v, tau, gain):
    R_out = core(q, k, v, tau, gain)
    words, scales = planes(np.moveaxis(R_out, 2, 0).reshape(512, -1))
    return R_out, words, scales

@@ -1,0 +1,262 @@
+from contextlib import ExitStack
+
+import concourse.mybir as mybir
+from concourse.masks import make_identity
+
+N, D = 1024, 512
+FLOPS = 2 * (2 * N * D * D)
+
+F32 = mybir.dt.float32
+BF16 = mybir.dt.bfloat16
+U32 = mybir.dt.uint32
+I32 = mybir.dt.int32
+U8 = mybir.dt.uint8
+FP8X4 = mybir.dt.float8_e4m3fn_x4
+ALU = mybir.AluOpType
+ACT = mybir.ActivationFunctionType
+P = 128
+
+NB4 = False
+MANUAL = True
+ORDER = (
+    "ck D 00", "ck A 01", "zk D 00", "cq D 00", "cq A 02", "zk D 01", "zq D 00", "cq A 03",
+    "cq D 01", "S P 00", "zq D 02", "ck A 11", "ck D 10", "S P 02", "cq D 10", "zk D 10",
+    "cq A 11", "zq D 10", "zk D 11", "tv P 1", "cq A 13", "zq D 01", "S P 10", "zq D 11",
+    "zq D 03", "S P 01", "cq A 12", "ts D 0", "S P 11", "S P 03", "tv P 0", "zq D 13",
+    "cv A 1", "zq D 12", "ts D 1", "tv P 3", "ex A 0", "S P 12", "zv D 1", "cv A 0",
+    "S P 13", "rc D 0", "ts D 2", "tv P 2", "ex A 1", "zv D 0", "no A 0", "ts D 3",
+    "ex A 2", "tc P 0", "rc D 1", "no A 1", "tt D 0", "ex A 3", "rc D 2", "tc P 1",
+    "zc D 0", "A P 00", "no A 2", "tt D 1", "cv A 2", "rc D 3", "tc P 2", "zc D 1",
+    "no A 3", "tt D 2", "A P 10", "cv A 3", "zv D 2", "tc P 3", "zc D 2", "ca A 00",
+    "tt D 3", "ca A 10", "zv D 3", "A P 20", "zc D 3", "A P 01", "ca A 20", "ob D 00",
+    "st S 00", "A P 31", "ob D 10", "A P 30", "A P 11", "ca A 01", "ca D 31", "st S 10",
+    "ob D 20", "ca A 11", "A P 21", "st S 20", "ob D 01", "ob D 31", "ca A 30", "st S 31",
+    "A P 33", "ob D 11", "st S 01", "A P 32", "ca A 21", "wt P 1", "ca D 33", "st S 11",
+    "ob D 30", "ca A 32", "ob D 33", "wt P 0", "st S 30", "ob D 21", "cw D 1", "st S 33",
+    "wt P 3", "st S 21", "cw A 0", "ob D 32", "st S 32", "zw D 1", "wt P 2", "cw D 3",
+    "cw A 2", "zw D 0", "sw S 1", "zw D 3", "zw D 2", "sw S 0", "sw S 3", "sw S 2",
+)
+
+
+def tile_scaledchannelattentioncentredmap_kernel(tc, q, k, v, tau, gain, out_0, out_1, out_2):
+    nc = tc.nc
+    with ExitStack() as ctx:
+        keep = ctx.enter_context(tc.tile_pool(name="keep", bufs=1))
+        psum = ctx.enter_context(tc.psum_pool(name="psum", bufs=1))
+        if MANUAL:
+            ctx.enter_context(tc.manual_schedule())
+        tiles = {}
+
+        def sb(name, shape, dtype):
+            if name not in tiles:
+                tiles[name] = keep.tile(shape, dtype, name=name, tag=name, align_bytes=64)
+            return tiles[name]
+
+        def bank(name, n):
+            if name not in tiles:
+                tiles[name] = psum.tile([P, 512], F32, name=name, tag="bank%d" % n)
+            return tiles[name]
+
+        def mx(out, lc, ls, lcols, rc, rs, rcols, start, stop):
+            nc.tensor.matmul_mx(
+                out=out,
+                lhsT=lc[:, lcols].bitcast(FP8X4), lhsT_scale=ls[:, lcols],
+                rhs=rc[:, rcols].bitcast(FP8X4), rhs_scale=rs[:, rcols],
+                start=start, stop=stop)
+
+        def copy(e, out, in_):
+            if e == "D":
+                nc.vector.tensor_copy(out=out, in_=in_)
+            else:
+                nc.scalar.copy(out=out, in_=in_)
+
+        taub = sb("taub", [4, P], BF16)
+        gain4 = sb("gain4", [P, 4], BF16)
+        nc.scalar.dma_start(out=taub[:], in_=tau.rearrange("(b p) -> b p", b=4))
+        nc.scalar.dma_start(out=gain4[:], in_=gain.rearrange("(p t) -> p t", t=4))
+        raw = {}
+        for g in range(2):
+            for x, src in (("k", k), ("q", q)):
+                t = sb("%sraw%d" % (x, g), [P, 4, D], BF16)
+                s3 = src[0, 512 * g:512 * g + 512, :].rearrange("(p j) w -> p j w", j=4)
+                if x == "k" and g == 0:
+                    nc.sync.dma_start(out=t[:, :, 0:256], in_=s3[:, :, 0:256])
+                    nc.sync.dma_start(out=t[:, :, 256:512], in_=s3[:, :, 256:512])
+                else:
+                    nc.sync.dma_start(out=t[:], in_=s3)
+                raw[x, g] = t
+        for b in range(2):
+            t = sb("vraw%d" % b, [P, 2, 2, D], BF16)
+            nc.sync.dma_start(out=t[:], in_=v[0, 512 * b:512 * b + 512, :].rearrange("(c p r) w -> p c r w", c=2, r=2))
+            raw["v", b] = t
+
+        zero = sb("zero", [P, 1], F32)
+        nc.gpsimd.memset(zero[:], 0.0)
+        tz = sb("tz", [P, P], F32)
+        nc.gpsimd.memset(tz[:], 0.0)
+        warm = sb("warm", [P, 1], F32)
+        nc.scalar.activation(out=warm[:], in_=zero[:], func=ACT.Exp)
+        ident = sb("ident", [P, P], F32)
+        make_identity(nc, ident[:])
+        ntau = sb("ntau", [P, 4], F32)
+        nc.gpsimd.tensor_scalar(out=tz[0:4, :], in0=taub[:], scalar1=-1.0 / 32.0, scalar2=0.0, op0=ALU.mult, op1=ALU.add)
+        tp = bank("tp", 7)
+        nc.tensor.transpose(tp[:, 0:P], tz[:], ident[:])
+        nc.scalar.copy(out=ntau[:], in_=tp[:, 0:4])
+
+        def interleave(e, x, g, c0, c1, dst):
+            if NB4:
+                copy(e, dst[:].rearrange("p (c i) j -> p c j i", i=4),
+                     raw[x, g][:, :, c0:c1].rearrange("p j (c i) -> p c j i", i=4))
+            else:
+                copy(e, dst[:], raw[x, g][:, :, c0:c1].rearrange("p j c -> p c j"))
+
+        def quant(x, g, c0, c1, src):
+            nc.vector.quantize_mx(
+                out=sb("%sc%d" % (x, g), [P, D], U32)[:, c0:c1].bitcast(FP8X4),
+                scales=sb("%ss%d" % (x, g), [P, D], U8)[:, c0:c1],
+                in_=src[:].rearrange("p c j -> p (c j)"))
+
+        def ck(e, g, h):
+            interleave(e, "k", g, 256 * h, 256 * h + 256, sb("kg%d%d" % (g, h), [P, 256, 4], BF16))
+
+        def zk(e, g, h):
+            quant("k", g, 256 * h, 256 * h + 256, tiles["kg%d%d" % (g, h)])
+
+        def cq(e, g, h):
+            interleave(e, "q", g, P * h, P * h + P, sb("qg%d%d" % (g, h), [P, P, 4], BF16))
+
+        def zq(e, g, h):
+            quant("q", g, P * h, P * h + P, tiles["qg%d%d" % (g, h)])
+
+        def S(e, g, t):
+            mx(bank("s%d" % t, t)[:], tiles["qc%d" % g], tiles["qs%d" % g], slice(P * t, P * t + P),
+               tiles["kc%d" % g], tiles["ks%d" % g], slice(0, D), g == 0, g == 1)
+
+        def tv(e, b):
+            words = raw["v", b // 2][:, b % 2].rearrange("p r w -> p (r w)").bitcast(F32)
+            vp = bank("vp%d" % b, 4 + b)
+            for u in range(2):
+                for r in range(2):
+                    nc.tensor.transpose(vp[:, P * (2 * u + r):P * (2 * u + r) + P], words[:, 256 * r + u:256 * (r + 1):2], ident[:])
+
+        def cv(e, b):
+            vg = sb("vg%d" % b, [P, 256, 4], BF16)
+            copy(e, vg[:].rearrange("p c j -> p (c j)").bitcast(F32).rearrange("p (t r u) -> p t r u", r=2, u=2),
+                 tiles["vp%d" % b][:].rearrange("p (u r t) -> p t r u", u=2, r=2))
+
+        def zv(e, b):
+            nc.vector.quantize_mx(
+                out=sb("vc%d" % b, [P, 256], U32)[:].bitcast(FP8X4),
+                scales=sb("vs%d" % b, [P, 256], U8)[:],
+                in_=tiles["vg%d" % b][:].rearrange("p c j -> p (c j)"))
+
+        def ts(e, t):
+            nc.vector.tensor_scalar(
+                out=sb("lneg%d" % t, [P, 4, P], F32)[:], in0=tiles["s%d" % t][:].rearrange("p (m t) -> p t m", t=4),
+                scalar1=ntau[:, t:t + 1], scalar2=None, op0=ALU.mult, op1=ALU.min,
+                accum_out=sb("mn%d" % t, [P, 1], F32)[:])
+
+        def ex(e, t):
+            nc.scalar.activation(
+                out=sb("e%d" % t, [P, 4, P], F32)[:], in_=tiles["lneg%d" % t][:], func=ACT.Exp,
+                bias=tiles["mn%d" % t][:], scale=-1.0, accum_out=sb("sum%d" % t, [P, 1], F32)[:])
+
+        def rc(e, t):
+            nc.vector.reciprocal(out=sb("rs%d" % t, [P, 1], F32)[:], in_=tiles["sum%d" % t][:])
+
+        def no(e, t):
+            out, in_, rs = sb("c0%d" % t, [P, 4, P], F32), tiles["e%d" % t], tiles["rs%d" % t]
+            if e == "A":
+                nc.scalar.activation(out=out[:], in_=in_[:], func=ACT.Identity, bias=-1.0 / 512.0, scale=rs[:])
+            else:
+                eng = nc.vector if e == "D" else nc.gpsimd
+                eng.tensor_scalar(out=out[:], in0=in_[:], scalar1=rs[:], scalar2=-1.0 / 512.0, op0=ALU.mult, op1=ALU.add)
+
+        def trc(e, t):
+            ct = bank("ct%d" % t, t)
+            for u in range(4):
+                nc.tensor.transpose(ct[:, P * u:P * u + P], tiles["c0%d" % t][:, u, :], ident[:])
+
+        def tt(e, t):
+            nc.vector.tensor_tensor(
+                out=sb("cg%d" % t, [P, P, 4], BF16)[:], in0=tiles["ct%d" % t][:].rearrange("p (u i) -> p i u", u=4),
+                in1=gain4[:].unsqueeze(1).to_broadcast([P, P, 4]), op=ALU.mult)
+
+        def zc(e, t):
+            nc.vector.quantize_mx(
+                out=sb("cc", [P, D], U32)[:, P * t:P * t + P].bitcast(FP8X4),
+                scales=sb("cs", [P, D], U8)[:, P * t:P * t + P],
+                in_=tiles["cg%d" % t][:].rearrange("p c j -> p (c j)"))
+
+        def A(e, t, G):
+            if t == 3:
+                w, blocks = G, (0, 1)
+                pa = bank("a3%d" % (w // 2), 6 + w // 2)
+                for r in blocks:
+                    n = 2 * (w % 2) + r
+                    mx(pa[:, P * n:P * n + P], tiles["vc%d" % w], tiles["vs%d" % w], slice(P * r, P * r + P),
+                       tiles["cc"], tiles["cs"], slice(P * t, P * t + P), True, True)
+                return
+            pa = bank("a%d%d" % (t, G), 4 + (2 * t + G) % 4)
+            for n in range(4):
+                b, r = 2 * G + n // 2, n % 2
+                mx(pa[:, P * n:P * n + P], tiles["vc%d" % b], tiles["vs%d" % b], slice(P * r, P * r + P),
+                   tiles["cc"], tiles["cs"], slice(P * t, P * t + P), True, True)
+
+        def part(t, G):
+            if t == 3:
+                return G // 2, slice(2 * (G % 2), 2 * (G % 2) + 2), slice(256 * (G % 2), 256 * (G % 2) + 256)
+            return G, slice(0, 4), slice(0, 512)
+
+        def ca(e, t, G):
+            g, ns, cols = part(t, G)
+            o = sb("o%d" % g, [P, 4, D], F32)
+            copy(e, o[:, ns, P * t:P * t + P], tiles["a%d%d" % (t, g)][:, cols].rearrange("q (n i) -> q n i", i=P))
+
+        def ob(e, t, G):
+            g, ns, cols = part(t, G)
+            out = sb("ob%d" % g, [P, 4, D], BF16)[:, ns, P * t:P * t + P]
+            in_ = tiles["o%d" % g][:, ns, P * t:P * t + P]
+            if e == "G":
+                nc.gpsimd.tensor_scalar(out=out, in0=in_, scalar1=1.0, scalar2=0.0, op0=ALU.mult, op1=ALU.add)
+            else:
+                copy(e, out, in_)
+
+        def st(e, t, G):
+            g, ns, cols = part(t, G)
+            dst = out_0[0, 512 * g:512 * g + 512, P * t:P * t + P].rearrange("(n q) i -> q n i", n=4)
+            nc.sync.dma_start(out=dst[:, ns, :], in_=tiles["o%d" % g][:, ns, P * t:P * t + P])
+
+        def wt(e, w):
+            wp = bank("wp%d" % w, w)
+            for u in range(2):
+                for r in range(2):
+                    words = tiles["ob%d" % (w // 2)][:, 2 * (w % 2) + r, :].bitcast(F32)
+                    nc.tensor.transpose(wp[:, P * (2 * u + r):P * (2 * u + r) + P], words[:, u:256:2], ident[:])
+
+        def cw(e, w):
+            og = sb("og%d" % w, [P, 256, 4], BF16)
+            copy(e, og[:].rearrange("p c j -> p (c j)").bitcast(F32).rearrange("p (m u) -> p m u", u=2),
+                 tiles["wp%d" % w][:].rearrange("p (u m) -> p m u", u=2))
+
+        def zw(e, w):
+            nc.vector.quantize_mx(
+                out=sb("wc%d" % w, [P, 256], U32)[:].bitcast(FP8X4),
+                scales=sb("ws%d" % w, [P, 256], U8)[:],
+                in_=tiles["og%d" % w][:].rearrange("p c j -> p (c j)"))
+
+        words_out = out_1[0].rearrange("p m t -> p (m t)").bitcast(I32)
+        scales_out = out_2[0].bitcast(I32)
+
+        def sw(e, w):
+            nc.sync.dma_start(out=words_out[:, 256 * w:256 * w + 256], in_=tiles["wc%d" % w][:].bitcast(I32))
+            for r in range(4):
+                nc.sync.dma_start(out=scales_out[4 * r:4 * r + 4, 64 * w:64 * w + 64],
+                                  in_=tiles["ws%d" % w][32 * r:32 * r + 4, :].bitcast(I32))
+
+        steps = dict(ck=ck, zk=zk, cq=cq, zq=zq, S=S, tv=tv, cv=cv, zv=zv, ts=ts, ex=ex, rc=rc, no=no, tc=trc, tt=tt, zc=zc,
+                     A=A, ca=ca, ob=ob, st=st, wt=wt, cw=cw, zw=zw, sw=sw)
+        for item in ORDER:
+            f, e, ids = item.split(" ")
+            steps[f](e, *[int(i) for i in ids])

@@ -16,25 +16,27 @@ ALU = mybir.AluOpType
 ACT = mybir.ActivationFunctionType
 P = 128
 
-NB4 = False
+NB4 = True
 MANUAL = True
 ORDER = (
     "ck D 00", "ck A 01", "zk D 00", "cq D 00", "cq A 02", "zk D 01", "zq D 00", "cq A 03",
-    "cq D 01", "S P 00", "zq D 02", "ck A 11", "ck D 10", "S P 02", "cq D 10", "zk D 10",
-    "cq A 11", "zq D 10", "zk D 11", "tv P 1", "cq A 13", "zq D 01", "S P 10", "zq D 11",
-    "zq D 03", "S P 01", "cq A 12", "ts D 0", "S P 11", "S P 03", "tv P 0", "zq D 13",
-    "cv A 1", "zq D 12", "ts D 1", "tv P 3", "ex A 0", "S P 12", "zv D 1", "cv A 0",
-    "S P 13", "rc D 0", "ts D 2", "tv P 2", "ex A 1", "zv D 0", "no A 0", "ts D 3",
-    "ex A 2", "tc P 0", "rc D 1", "no A 1", "tt D 0", "ex A 3", "rc D 2", "tc P 1",
-    "zc D 0", "A P 00", "no A 2", "tt D 1", "cv A 2", "rc D 3", "tc P 2", "zc D 1",
-    "no A 3", "tt D 2", "A P 10", "cv A 3", "zv D 2", "tc P 3", "zc D 2", "ca A 00",
-    "tt D 3", "ca A 10", "zv D 3", "A P 20", "zc D 3", "A P 01", "ca A 20", "ob D 00",
-    "st S 00", "A P 31", "ob D 10", "A P 30", "A P 11", "ca A 01", "ca D 31", "st S 10",
-    "ob D 20", "ca A 11", "A P 21", "st S 20", "ob D 01", "ob D 31", "ca A 30", "st S 31",
-    "A P 33", "ob D 11", "st S 01", "A P 32", "ca A 21", "wt P 1", "ca D 33", "st S 11",
-    "ob D 30", "ca A 32", "ob D 33", "wt P 0", "st S 30", "ob D 21", "cw D 1", "st S 33",
-    "wt P 3", "st S 21", "cw A 0", "ob D 32", "st S 32", "zw D 1", "wt P 2", "cw D 3",
-    "cw A 2", "zw D 0", "sw S 1", "zw D 3", "zw D 2", "sw S 0", "sw S 3", "sw S 2",
+    "cq D 01", "S P 00", "zq D 02", "ck A 11", "zq D 01", "S P 02", "ck D 10", "S P 01",
+    "zq D 03", "cq D 10", "S P 03", "dm P 0", "dm P 0", "cq A 11", "zk D 11", "zq D 10",
+    "tv P 0", "cq A 12", "zk D 10", "zq D 11", "S P 10", "cq A 13", "S P 11", "zq D 12",
+    "ts D 0", "S P 12", "cv A 0", "tv P 1", "zq D 13", "ts D 1", "ex A 0", "S P 13",
+    "dm P 0", "dm P 0", "tv P 3", "cv A 1", "ts D 2", "tv P 2", "dm P 0", "ex A 1",
+    "rc D 0", "zv D 1", "cv D 3", "ex A 2", "rc D 1", "no A 0", "ts D 3", "no A 1",
+    "rc D 2", "tc P 0", "dm P 0", "dm P 0", "zv D 3", "zv D 0", "ex A 3", "tc P 1",
+    "dm P 0", "tt D 0", "no A 2", "rc D 3", "tt D 1", "no A 3", "tc P 2", "dm P 1",
+    "zc D 0", "cv A 2", "zc D 1", "A P 00", "tt D 2", "tc P 3", "dm P 1", "dm P 1",
+    "ca A 00", "zv D 2", "A P 10", "zc D 2", "A P 11", "tt D 3", "ca A 10", "A P 01",
+    "ob D 00", "ca A 11", "A P 20", "st S 00", "zc D 3", "ob D 10", "ca A 01", "A P 31",
+    "st S 10", "ob D 11", "A P 33", "A P 30", "ca D 31", "ca A 20", "A P 32", "A P 21",
+    "ca D 33", "ca A 30", "ob D 31", "st S 01", "ob D 20", "st S 11", "ca A 21", "ob D 33",
+    "ob D 30", "wt P 1", "ca A 32", "ob D 01", "st S 33", "ob D 21", "wt P 0", "st S 30",
+    "cw D 1", "st S 31", "st S 20", "wt P 3", "ob D 32", "cw A 0", "st S 32", "zw D 1",
+    "wt P 2", "st S 21", "cw D 3", "zw D 0", "cw A 2", "sw S 1", "zw D 3", "zw D 2",
+    "sw S 0", "sw S 3", "sw S 2",
 )
 
 
@@ -135,7 +137,7 @@ def tile_scaledchannelattentioncentredmap_kernel(tc, q, k, v, tau, gain, out_0, 
 
         def tv(e, b):
             words = raw["v", b // 2][:, b % 2].rearrange("p r w -> p (r w)").bitcast(F32)
-            vp = bank("vp%d" % b, 4 + b)
+            vp = bank("vp%d" % b, (4, 5, 6, 4)[b])
             for u in range(2):
                 for r in range(2):
                     nc.tensor.transpose(vp[:, P * (2 * u + r):P * (2 * u + r) + P], words[:, 256 * r + u:256 * (r + 1):2], ident[:])
@@ -225,8 +227,11 @@ def tile_scaledchannelattentioncentredmap_kernel(tc, q, k, v, tau, gain, out_0, 
 
         def st(e, t, G):
             g, ns, cols = part(t, G)
-            dst = out_0[0, 512 * g:512 * g + 512, P * t:P * t + P].rearrange("(n q) i -> q n i", n=4)
-            nc.sync.dma_start(out=dst[:, ns, :], in_=tiles["o%d" % g][:, ns, P * t:P * t + P])
+            if t == 0:
+                return
+            i0 = 0 if t == 1 else P * t
+            dst = out_0[0, 512 * g:512 * g + 512, i0:P * t + P].rearrange("(n q) i -> q n i", n=4)
+            nc.sync.dma_start(out=dst[:, ns, :], in_=tiles["o%d" % g][:, ns, i0:P * t + P])
 
         def wt(e, w):
             wp = bank("wp%d" % w, w)
@@ -243,7 +248,7 @@ def tile_scaledchannelattentioncentredmap_kernel(tc, q, k, v, tau, gain, out_0, 
         def zw(e, w):
             nc.vector.quantize_mx(
                 out=sb("wc%d" % w, [P, 256], U32)[:].bitcast(FP8X4),
-                scales=sb("ws%d" % w, [P, 256], U8)[:],
+                scales=sb("ws", [P, 1024], U8)[:, 256 * w:256 * w + 256],
                 in_=tiles["og%d" % w][:].rearrange("p c j -> p (c j)"))
 
         words_out = out_1[0].rearrange("p m t -> p (m t)").bitcast(I32)
@@ -251,12 +256,15 @@ def tile_scaledchannelattentioncentredmap_kernel(tc, q, k, v, tau, gain, out_0, 
 
         def sw(e, w):
             nc.sync.dma_start(out=words_out[:, 256 * w:256 * w + 256], in_=tiles["wc%d" % w][:].bitcast(I32))
-            for r in range(4):
-                nc.sync.dma_start(out=scales_out[4 * r:4 * r + 4, 64 * w:64 * w + 64],
-                                  in_=tiles["ws%d" % w][32 * r:32 * r + 4, :].bitcast(I32))
 
-        steps = dict(ck=ck, zk=zk, cq=cq, zq=zq, S=S, tv=tv, cv=cv, zv=zv, ts=ts, ex=ex, rc=rc, no=no, tc=trc, tt=tt, zc=zc,
+        def dm(e, n):
+            mx(bank("dm%d" % n, 7 if n == 0 else 0)[:], tiles["kc0"], tiles["ks0"], slice(0, P), tiles["kc0"], tiles["ks0"], slice(0, D), True, True)
+
+        steps = dict(dm=dm, ck=ck, zk=zk, cq=cq, zq=zq, S=S, tv=tv, cv=cv, zv=zv, ts=ts, ex=ex, rc=rc, no=no, tc=trc, tt=tt, zc=zc,
                      A=A, ca=ca, ob=ob, st=st, wt=wt, cw=cw, zw=zw, sw=sw)
         for item in ORDER:
             f, e, ids = item.split(" ")
             steps[f](e, *[int(i) for i in ids])
+        for r in range(4):
+            eng = nc.sync if r % 2 else nc.scalar
+            eng.dma_start(out=scales_out[4 * r:4 * r + 4, :], in_=tiles["ws"][32 * r:32 * r + 4, :].bitcast(I32))

@@ -19,24 +19,22 @@ P = 128
 NB4 = True
 MANUAL = True
 ORDER = (
-    "ck D 00", "ck A 01", "zk D 00", "cq D 00", "cq A 02", "zk D 01", "zq D 00", "cq A 03",
-    "cq D 01", "S P 00", "zq D 02", "ck A 11", "zq D 01", "S P 02", "ck D 10", "S P 01",
-    "zq D 03", "cq D 10", "S P 03", "dm P 0", "dm P 0", "cq A 11", "zk D 11", "zq D 10",
-    "tv P 0", "cq A 12", "zk D 10", "zq D 11", "S P 10", "cq A 13", "S P 11", "zq D 12",
-    "ts D 0", "S P 12", "cv A 0", "tv P 1", "zq D 13", "ts D 1", "ex A 0", "S P 13",
-    "dm P 0", "dm P 0", "tv P 3", "cv A 1", "ts D 2", "tv P 2", "dm P 0", "ex A 1",
-    "rc D 0", "zv D 1", "cv D 3", "ex A 2", "rc D 1", "no A 0", "ts D 3", "no A 1",
-    "rc D 2", "tc P 0", "dm P 0", "dm P 0", "zv D 3", "zv D 0", "ex A 3", "tc P 1",
-    "dm P 0", "tt D 0", "no A 2", "rc D 3", "tt D 1", "no A 3", "tc P 2", "dm P 1",
-    "zc D 0", "cv A 2", "zc D 1", "A P 00", "tt D 2", "tc P 3", "dm P 1", "dm P 1",
-    "ca A 00", "zv D 2", "A P 10", "zc D 2", "A P 11", "tt D 3", "ca A 10", "A P 01",
-    "ob D 00", "ca A 11", "A P 20", "st S 00", "zc D 3", "ob D 10", "ca A 01", "A P 31",
-    "st S 10", "ob D 11", "A P 33", "A P 30", "ca D 31", "ca A 20", "A P 32", "A P 21",
-    "ca D 33", "ca A 30", "ob D 31", "st S 01", "ob D 20", "st S 11", "ca A 21", "ob D 33",
-    "ob D 30", "wt P 1", "ca A 32", "ob D 01", "st S 33", "ob D 21", "wt P 0", "st S 30",
-    "cw D 1", "st S 31", "st S 20", "wt P 3", "ob D 32", "cw A 0", "st S 32", "zw D 1",
-    "wt P 2", "st S 21", "cw D 3", "zw D 0", "cw A 2", "sw S 1", "zw D 3", "zw D 2",
-    "sw S 0", "sw S 3", "sw S 2",
+    "ck D 00", "ck A 01", "zk D 00", "cq D 02", "cq A 01", "cq D 03", "zk D 01", "cq A 00",
+    "zq D 03", "zq D 01", "zq D 02", "ck A 11", "S P 03", "zq D 00", "S P 01", "ck D 10",
+    "S P 02", "S P 00", "cq D 11", "dm P 0", "cq A 10", "zk D 11", "zk D 10", "cq A 13",
+    "tv P 1", "zq D 10", "cq D 12", "zq D 11", "S P 10", "zq D 12", "cv A 1", "zq D 13",
+    "S P 11", "ts D 0", "S P 12", "tv P 0", "ts D 1", "ex A 0", "S P 13", "ts D 2",
+    "cv A 0", "tv P 2", "rc D 0", "ts D 3", "ex A 1", "tv P 3", "no D 0", "ex A 2",
+    "rc D 1", "zv D 0", "tc P 0", "ex A 3", "no D 1", "rc D 2", "zv D 1", "cv A 2",
+    "tc P 1", "tt D 0", "dm P 0", "no A 2", "rc D 3", "tt D 1", "no A 3", "zv D 2",
+    "tc P 2", "cv A 3", "zc D 1", "zc D 0", "tc P 3", "tt D 2", "A P 01", "tt D 3",
+    "A P 00", "A P 02", "ca A 01", "zv D 3", "zc D 3", "ca A 00", "zc D 2", "A P 03",
+    "shA D ", "shB D ", "A P 11", "ca A 02", "ca D 03", "A P 10", "ca A 11", "B P 1",
+    "st S 01", "ca D 10", "A P 12", "A P 13", "cb A 1", "st S 00", "B P 2", "ca A 12",
+    "B P 4", "ca D 13", "st S 02", "B P 3", "cb D 2", "B P 0", "cb A 4", "st S 11",
+    "B P 7", "cb D 3", "cb A 0", "B P 6", "st S 10", "B P 5", "cb D 7", "cb A 6",
+    "st S 12", "zw D 0", "cb A 5", "zw D 1", "st S 03", "zw D 3", "st S 13", "zw D 2",
+    "sw S 0", "sw S 1", "sw S 3", "sw S 2",
 )
 
 
@@ -74,8 +72,6 @@ def tile_scaledchannelattentioncentredmap_kernel(tc, q, k, v, tau, gain, out_0, 
 
         taub = sb("taub", [4, P], BF16)
         gain4 = sb("gain4", [P, 4], BF16)
-        nc.scalar.dma_start(out=taub[:], in_=tau.rearrange("(b p) -> b p", b=4))
-        nc.scalar.dma_start(out=gain4[:], in_=gain.rearrange("(p t) -> p t", t=4))
         raw = {}
         for g in range(2):
             for x, src in (("k", k), ("q", q)):
@@ -95,9 +91,14 @@ def tile_scaledchannelattentioncentredmap_kernel(tc, q, k, v, tau, gain, out_0, 
         zero = sb("zero", [P, 1], F32)
         nc.gpsimd.memset(zero[:], 0.0)
         tz = sb("tz", [P, P], F32)
+        cc, cs = sb("cc", [P, D], U32), sb("cs", [P, D], U8)
+        dc, ds = sb("dc", [P, D], U32), sb("ds", [P, D], U8)
+        nc.gpsimd.memset(cs[:].bitcast(I32), 0)
         nc.gpsimd.memset(tz[:], 0.0)
         warm = sb("warm", [P, 1], F32)
         nc.scalar.activation(out=warm[:], in_=zero[:], func=ACT.Exp)
+        nc.scalar.dma_start(out=taub[:], in_=tau.rearrange("(b p) -> b p", b=4))
+        nc.scalar.dma_start(out=gain4[:], in_=gain.rearrange("(p t) -> p t", t=4))
         ident = sb("ident", [P, P], F32)
         make_identity(nc, ident[:])
         ntau = sb("ntau", [P, 4], F32)
@@ -182,68 +183,51 @@ def tile_scaledchannelattentioncentredmap_kernel(tc, q, k, v, tau, gain, out_0, 
 
         def tt(e, t):
             nc.vector.tensor_tensor(
-                out=sb("cg%d" % t, [P, P, 4], BF16)[:], in0=tiles["ct%d" % t][:].rearrange("p (u i) -> p i u", u=4),
-                in1=gain4[:].unsqueeze(1).to_broadcast([P, P, 4]), op=ALU.mult)
+                out=sb("cg%d" % t, [P, 4, 32, 4], BF16)[:],
+                in0=tiles["ct%d" % t][:].rearrange("p (u m t) -> p t m u", u=4, t=4),
+                in1=gain4[:].unsqueeze(1).unsqueeze(1).to_broadcast([P, 4, 32, 4]), op=ALU.mult)
 
         def zc(e, t):
             nc.vector.quantize_mx(
-                out=sb("cc", [P, D], U32)[:, P * t:P * t + P].bitcast(FP8X4),
-                scales=sb("cs", [P, D], U8)[:, P * t:P * t + P],
-                in_=tiles["cg%d" % t][:].rearrange("p c j -> p (c j)"))
+                out=cc[:, P * t:P * t + P].bitcast(FP8X4), scales=cs[:, P * t:P * t + P],
+                in_=tiles["cg%d" % t][:].rearrange("p t m j -> p (t m j)"))
 
-        def A(e, t, G):
-            if t == 3:
-                w, blocks = G, (0, 1)
-                pa = bank("a3%d" % (w // 2), 6 + w // 2)
-                for r in blocks:
-                    n = 2 * (w % 2) + r
-                    mx(pa[:, P * n:P * n + P], tiles["vc%d" % w], tiles["vs%d" % w], slice(P * r, P * r + P),
-                       tiles["cc"], tiles["cs"], slice(P * t, P * t + P), True, True)
-                return
-            pa = bank("a%d%d" % (t, G), 4 + (2 * t + G) % 4)
-            for n in range(4):
-                b, r = 2 * G + n // 2, n % 2
-                mx(pa[:, P * n:P * n + P], tiles["vc%d" % b], tiles["vs%d" % b], slice(P * r, P * r + P),
-                   tiles["cc"], tiles["cs"], slice(P * t, P * t + P), True, True)
+        def sh(e, h):
+            for src, dst, w in ((cc, dc, 32), (cs, ds, 8)):
+                nc.vector.tensor_copy(
+                    out=dst[:].bitcast(I32).rearrange("p (t b m) -> p t b m", t=4, b=4)[:, :, 2 * h:2 * h + 2, :],
+                    in_=src[:].bitcast(I32).rearrange("p (b t m) -> p t b m", t=4, b=4)[:, :, 2 * h:2 * h + 2, :])
 
-        def part(t, G):
-            if t == 3:
-                return G // 2, slice(2 * (G % 2), 2 * (G % 2) + 2), slice(256 * (G % 2), 256 * (G % 2) + 256)
-            return G, slice(0, 4), slice(0, 512)
+        def shA(e):
+            sh(e, 0)
 
-        def ca(e, t, G):
-            g, ns, cols = part(t, G)
-            o = sb("o%d" % g, [P, 4, D], F32)
-            copy(e, o[:, ns, P * t:P * t + P], tiles["a%d%d" % (t, g)][:, cols].rearrange("q (n i) -> q n i", i=P))
+        def shB(e):
+            sh(e, 1)
 
-        def ob(e, t, G):
-            g, ns, cols = part(t, G)
-            out = sb("ob%d" % g, [P, 4, D], BF16)[:, ns, P * t:P * t + P]
-            in_ = tiles["o%d" % g][:, ns, P * t:P * t + P]
-            if e == "G":
-                nc.gpsimd.tensor_scalar(out=out, in0=in_, scalar1=1.0, scalar2=0.0, op0=ALU.mult, op1=ALU.add)
-            else:
-                copy(e, out, in_)
+        def A(e, h, m):
+            pa = bank("a%d%d" % (h, m), (5, 6, 7, 4)[m])
+            for r in range(2):
+                mx(pa[:, 256 * r:256 * r + 256], tiles["vc%d" % m], tiles["vs%d" % m], slice(P * r, P * r + P),
+                   cc, cs, slice(256 * h, 256 * h + 256), True, True)
 
-        def st(e, t, G):
-            g, ns, cols = part(t, G)
-            if t == 0:
-                return
-            i0 = 0 if t == 1 else P * t
-            dst = out_0[0, 512 * g:512 * g + 512, i0:P * t + P].rearrange("(n q) i -> q n i", n=4)
-            nc.sync.dma_start(out=dst[:, ns, :], in_=tiles["o%d" % g][:, ns, i0:P * t + P])
+        def ca(e, h, m):
+            copy(e, sb("o%d%d" % (h, m), [P, 2, 256], F32)[:].rearrange("q n (b m t) -> q (n b) m t", b=2, t=4),
+                 tiles["a%d%d" % (h, m)][:].rearrange("q (c t m) -> q c m t", c=4, t=4))
 
-        def wt(e, w):
-            wp = bank("wp%d" % w, w)
-            for u in range(2):
-                for r in range(2):
-                    words = tiles["ob%d" % (w // 2)][:, 2 * (w % 2) + r, :].bitcast(F32)
-                    nc.tensor.transpose(wp[:, P * (2 * u + r):P * (2 * u + r) + P], words[:, u:256:2], ident[:])
+        def st(e, h, m):
+            nc.sync.dma_start(
+                out=out_0[0, 256 * m:256 * m + 256, 256 * h:256 * h + 256].rearrange("(n q) i -> q n i", n=2),
+                in_=tiles["o%d%d" % (h, m)][:])
 
-        def cw(e, w):
-            og = sb("og%d" % w, [P, 256, 4], BF16)
-            copy(e, og[:].rearrange("p c j -> p (c j)").bitcast(F32).rearrange("p (m u) -> p m u", u=2),
-                 tiles["wp%d" % w][:].rearrange("p (u m) -> p m u", u=2))
+        def B(e, n):
+            pb = bank("b%d" % n, (0, 1, 2, 3, 5, 6, 7, 4)[n])
+            for t in range(4):
+                mx(pb[:, P * t:P * t + P], dc, ds, slice(P * t, P * t + P),
+                   tiles["vc%d" % (n // 2)], tiles["vs%d" % (n // 2)], slice(P * (n % 2), P * (n % 2) + P), True, True)
+
+        def cb(e, n):
+            copy(e, sb("og%d" % (n // 2), [P, 256, 4], BF16)[:, P * (n % 2):P * (n % 2) + P, :],
+                 tiles["b%d" % n][:].rearrange("p (t m) -> p m t", t=4))
 
         def zw(e, w):
             nc.vector.quantize_mx(
@@ -258,10 +242,10 @@ def tile_scaledchannelattentioncentredmap_kernel(tc, q, k, v, tau, gain, out_0, 
             nc.sync.dma_start(out=words_out[:, 256 * w:256 * w + 256], in_=tiles["wc%d" % w][:].bitcast(I32))
 
         def dm(e, n):
-            mx(bank("dm%d" % n, 7 if n == 0 else 0)[:], tiles["kc0"], tiles["ks0"], slice(0, P), tiles["kc0"], tiles["ks0"], slice(0, D), True, True)
+            mx(bank("dm", 7)[:], tiles["kc0"], tiles["ks0"], slice(0, P), tiles["kc0"], tiles["ks0"], slice(0, D), True, True)
 
         steps = dict(dm=dm, ck=ck, zk=zk, cq=cq, zq=zq, S=S, tv=tv, cv=cv, zv=zv, ts=ts, ex=ex, rc=rc, no=no, tc=trc, tt=tt, zc=zc,
-                     A=A, ca=ca, ob=ob, st=st, wt=wt, cw=cw, zw=zw, sw=sw)
+                     A=A, ca=ca, st=st, B=B, cb=cb, shA=shA, shB=shB, zw=zw, sw=sw)
         for item in ORDER:
             f, e, ids = item.split(" ")
             steps[f](e, *[int(i) for i in ids])

@@ -19,22 +19,23 @@ P = 128
 NB4 = True
 MANUAL = True
 ORDER = (
-    "ck D 00", "ck A 01", "zk D 00", "cq D 02", "cq A 01", "cq D 03", "zk D 01", "cq A 00",
-    "zq D 03", "zq D 01", "zq D 02", "ck A 11", "S P 03", "zq D 00", "S P 01", "ck D 10",
-    "S P 02", "S P 00", "cq D 11", "dm P 0", "cq A 10", "zk D 11", "zk D 10", "cq A 13",
-    "tv P 1", "zq D 10", "cq D 12", "zq D 11", "S P 10", "zq D 12", "cv A 1", "zq D 13",
-    "S P 11", "ts D 0", "S P 12", "tv P 0", "ts D 1", "ex A 0", "S P 13", "ts D 2",
-    "cv A 0", "tv P 2", "rc D 0", "ts D 3", "ex A 1", "tv P 3", "no D 0", "ex A 2",
-    "rc D 1", "zv D 0", "tc P 0", "ex A 3", "no D 1", "rc D 2", "zv D 1", "cv A 2",
-    "tc P 1", "tt D 0", "dm P 0", "no A 2", "rc D 3", "tt D 1", "no A 3", "zv D 2",
-    "tc P 2", "cv A 3", "zc D 1", "zc D 0", "tc P 3", "tt D 2", "A P 01", "tt D 3",
-    "A P 00", "A P 02", "ca A 01", "zv D 3", "zc D 3", "ca A 00", "zc D 2", "A P 03",
-    "shA D ", "shB D ", "A P 11", "ca A 02", "ca D 03", "A P 10", "ca A 11", "B P 1",
-    "st S 01", "ca D 10", "A P 12", "A P 13", "cb A 1", "st S 00", "B P 2", "ca A 12",
-    "B P 4", "ca D 13", "st S 02", "B P 3", "cb D 2", "B P 0", "cb A 4", "st S 11",
-    "B P 7", "cb D 3", "cb A 0", "B P 6", "st S 10", "B P 5", "cb D 7", "cb A 6",
-    "st S 12", "zw D 0", "cb A 5", "zw D 1", "st S 03", "zw D 3", "st S 13", "zw D 2",
-    "sw S 0", "sw S 1", "sw S 3", "sw S 2",
+    "ck D 00", "ck D 01", "zk D 00", "zk D 01", "cq A 00", "cq D 01", "cq D 02", "cq A 03",
+    "zq D 01", "ck D 10", "ck A 11", "S P 01", "dm P 0", "zq D 00", "zq D 02", "zk D 10",
+    "S P 00", "cq D 13", "cq A 11", "S P 02", "cq D 12", "dm P 0", "zk D 11", "cq A 10",
+    "tau P ", "tv P 0", "zq D 11", "zq D 12", "zq D 03", "S P 11", "zq D 10", "cv A 0",
+    "zq D 13", "S P 12", "S P 10", "ts D 1", "S P 03", "S P 13", "ts D 0", "dm P 0",
+    "dm P 0", "tv P 1", "ex A 1", "ts D 2", "tv P 3", "ex A 0", "rc D 1", "ts D 3",
+    "tv P 2", "ex A 2", "rc D 0", "no D 1", "dm P 0", "ex A 3", "zv D 0", "rc D 2",
+    "tc P 1", "no D 0", "cv A 3", "no D 2", "tc P 0", "rc D 3", "tt D 1", "cv A 1",
+    "tc P 2", "no A 3", "tt D 0", "dm P 0", "dm P 0", "cv A 2", "zc D 1", "tc P 3",
+    "zc D 0", "zv D 1", "zv D 3", "A P 00", "tt D 2", "A P 01", "ca A 00", "A P 03",
+    "tt D 3", "ca A 01", "zv D 2", "ca A 03", "zc D 2", "zc D 3", "A P 02", "shA D ",
+    "shB D ", "A P 10", "st S 00", "ca A 02", "A P 11", "B P 2", "ca D 10", "st S 01",
+    "ca A 11", "A P 13", "A P 12", "cb D 2", "st S 03", "B P 3", "ca A 13", "B P 1",
+    "ca D 12", "st S 02", "cb A 3", "B P 4", "cb D 1", "B P 7", "cb A 4", "B P 5",
+    "st S 10", "zw D 1", "B P 0", "cb D 7", "cb A 5", "B P 6", "st S 13", "cb D 0",
+    "cb A 6", "st S 12", "zw D 2", "zw D 0", "sw S 1", "zw D 3", "st S 11", "sw S 2",
+    "sw S 0", "sw S 3",
 )
 
 
@@ -72,6 +73,7 @@ def tile_scaledchannelattentioncentredmap_kernel(tc, q, k, v, tau, gain, out_0, 
 
         taub = sb("taub", [4, P], BF16)
         gain4 = sb("gain4", [P, 4], BF16)
+        nc.scalar.dma_start(out=taub[:], in_=tau.rearrange("(b p) -> b p", b=4))
         raw = {}
         for g in range(2):
             for x, src in (("k", k), ("q", q)):
@@ -97,15 +99,15 @@ def tile_scaledchannelattentioncentredmap_kernel(tc, q, k, v, tau, gain, out_0, 
         nc.gpsimd.memset(tz[:], 0.0)
         warm = sb("warm", [P, 1], F32)
         nc.scalar.activation(out=warm[:], in_=zero[:], func=ACT.Exp)
-        nc.scalar.dma_start(out=taub[:], in_=tau.rearrange("(b p) -> b p", b=4))
         nc.scalar.dma_start(out=gain4[:], in_=gain.rearrange("(p t) -> p t", t=4))
         ident = sb("ident", [P, P], F32)
         make_identity(nc, ident[:])
         ntau = sb("ntau", [P, 4], F32)
         nc.gpsimd.tensor_scalar(out=tz[0:4, :], in0=taub[:], scalar1=-1.0 / 32.0, scalar2=0.0, op0=ALU.mult, op1=ALU.add)
-        tp = bank("tp", 7)
-        nc.tensor.transpose(tp[:, 0:P], tz[:], ident[:])
-        nc.scalar.copy(out=ntau[:], in_=tp[:, 0:4])
+        def tau_(e):
+            tp = bank("tp", 6)
+            nc.tensor.transpose(tp[:, 0:P], tz[:], ident[:])
+            nc.scalar.copy(out=ntau[:], in_=tp[:, 0:4])
 
         def interleave(e, x, g, c0, c1, dst):
             if NB4:
@@ -245,7 +247,7 @@ def tile_scaledchannelattentioncentredmap_kernel(tc, q, k, v, tau, gain, out_0, 
             mx(bank("dm", 7)[:], tiles["kc0"], tiles["ks0"], slice(0, P), tiles["kc0"], tiles["ks0"], slice(0, D), True, True)
 
         steps = dict(dm=dm, ck=ck, zk=zk, cq=cq, zq=zq, S=S, tv=tv, cv=cv, zv=zv, ts=ts, ex=ex, rc=rc, no=no, tc=trc, tt=tt, zc=zc,
-                     A=A, ca=ca, st=st, B=B, cb=cb, shA=shA, shB=shB, zw=zw, sw=sw)
+                     tau=tau_, A=A, ca=ca, st=st, B=B, cb=cb, shA=shA, shB=shB, zw=zw, sw=sw)
         for item in ORDER:
             f, e, ids = item.split(" ")
             steps[f](e, *[int(i) for i in ids])

from contextlib import ExitStack

import concourse.mybir as mybir
from concourse.masks import make_identity

N, D = 1024, 512
FLOPS = 2 * (2 * N * D * D)

F32 = mybir.dt.float32
BF16 = mybir.dt.bfloat16
U32 = mybir.dt.uint32
I32 = mybir.dt.int32
U8 = mybir.dt.uint8
FP8X4 = mybir.dt.float8_e4m3fn_x4
ALU = mybir.AluOpType
ACT = mybir.ActivationFunctionType
P = 128

NB4 = True
MANUAL = True
ORDER = (
    "ck D 00", "ck D 01", "zk D 00", "zk D 01", "cq A 00", "cq D 01", "cq D 02", "cq A 03",
    "zq D 01", "ck D 10", "ck A 11", "S P 01", "dm P 0", "zq D 00", "zq D 02", "zk D 10",
    "S P 00", "cq D 13", "cq A 11", "S P 02", "cq D 12", "dm P 0", "zk D 11", "cq A 10",
    "tau P ", "tv P 0", "zq D 11", "zq D 12", "zq D 03", "S P 11", "zq D 10", "cv A 0",
    "zq D 13", "S P 12", "S P 10", "ts D 1", "S P 03", "S P 13", "ts D 0", "dm P 0",
    "dm P 0", "tv P 1", "ex A 1", "ts D 2", "tv P 3", "ex A 0", "rc D 1", "ts D 3",
    "tv P 2", "ex A 2", "rc D 0", "no D 1", "dm P 0", "ex A 3", "zv D 0", "rc D 2",
    "tc P 1", "no D 0", "cv A 3", "no D 2", "tc P 0", "rc D 3", "tt D 1", "cv A 1",
    "tc P 2", "no A 3", "tt D 0", "dm P 0", "dm P 0", "cv A 2", "zc D 1", "tc P 3",
    "zc D 0", "zv D 1", "zv D 3", "A P 00", "tt D 2", "A P 01", "ca A 00", "A P 03",
    "tt D 3", "ca A 01", "zv D 2", "ca A 03", "zc D 2", "zc D 3", "A P 02", "shA D ",
    "shB D ", "A P 10", "st S 00", "ca A 02", "A P 11", "B P 2", "ca D 10", "st S 01",
    "ca A 11", "A P 13", "A P 12", "cb D 2", "st S 03", "B P 3", "ca A 13", "B P 1",
    "ca D 12", "st S 02", "cb A 3", "B P 4", "cb D 1", "B P 7", "cb A 4", "B P 5",
    "st S 10", "zw D 1", "B P 0", "cb D 7", "cb A 5", "B P 6", "st S 13", "cb D 0",
    "cb A 6", "st S 12", "zw D 2", "zw D 0", "sw S 1", "zw D 3", "st S 11", "sw S 2",
    "sw S 0", "sw S 3",
)


def tile_scaledchannelattentioncentredmap_kernel(tc, q, k, v, tau, gain, out_0, out_1, out_2):
    nc = tc.nc
    with ExitStack() as ctx:
        keep = ctx.enter_context(tc.tile_pool(name="keep", bufs=1))
        psum = ctx.enter_context(tc.psum_pool(name="psum", bufs=1))
        if MANUAL:
            ctx.enter_context(tc.manual_schedule())
        tiles = {}

        def sb(name, shape, dtype):
            if name not in tiles:
                tiles[name] = keep.tile(shape, dtype, name=name, tag=name, align_bytes=64)
            return tiles[name]

        def bank(name, n):
            if name not in tiles:
                tiles[name] = psum.tile([P, 512], F32, name=name, tag="bank%d" % n)
            return tiles[name]

        def mx(out, lc, ls, lcols, rc, rs, rcols, start, stop):
            nc.tensor.matmul_mx(
                out=out,
                lhsT=lc[:, lcols].bitcast(FP8X4), lhsT_scale=ls[:, lcols],
                rhs=rc[:, rcols].bitcast(FP8X4), rhs_scale=rs[:, rcols],
                start=start, stop=stop)

        def copy(e, out, in_):
            if e == "D":
                nc.vector.tensor_copy(out=out, in_=in_)
            else:
                nc.scalar.copy(out=out, in_=in_)

        taub = sb("taub", [4, P], BF16)
        gain4 = sb("gain4", [P, 4], BF16)
        nc.scalar.dma_start(out=taub[:], in_=tau.rearrange("(b p) -> b p", b=4))
        raw = {}
        for g in range(2):
            for x, src in (("k", k), ("q", q)):
                t = sb("%sraw%d" % (x, g), [P, 4, D], BF16)
                s3 = src[0, 512 * g:512 * g + 512, :].rearrange("(p j) w -> p j w", j=4)
                if x == "k" and g == 0:
                    nc.sync.dma_start(out=t[:, :, 0:256], in_=s3[:, :, 0:256])
                    nc.sync.dma_start(out=t[:, :, 256:512], in_=s3[:, :, 256:512])
                else:
                    nc.sync.dma_start(out=t[:], in_=s3)
                raw[x, g] = t
        for b in range(2):
            t = sb("vraw%d" % b, [P, 2, 2, D], BF16)
            nc.sync.dma_start(out=t[:], in_=v[0, 512 * b:512 * b + 512, :].rearrange("(c p r) w -> p c r w", c=2, r=2))
            raw["v", b] = t

        zero = sb("zero", [P, 1], F32)
        nc.gpsimd.memset(zero[:], 0.0)
        tz = sb("tz", [P, P], F32)
        cc, cs = sb("cc", [P, D], U32), sb("cs", [P, D], U8)
        dc, ds = sb("dc", [P, D], U32), sb("ds", [P, D], U8)
        nc.gpsimd.memset(cs[:].bitcast(I32), 0)
        nc.gpsimd.memset(tz[:], 0.0)
        warm = sb("warm", [P, 1], F32)
        nc.scalar.activation(out=warm[:], in_=zero[:], func=ACT.Exp)
        nc.scalar.dma_start(out=gain4[:], in_=gain.rearrange("(p t) -> p t", t=4))
        ident = sb("ident", [P, P], F32)
        make_identity(nc, ident[:])
        ntau = sb("ntau", [P, 4], F32)
        nc.gpsimd.tensor_scalar(out=tz[0:4, :], in0=taub[:], scalar1=-1.0 / 32.0, scalar2=0.0, op0=ALU.mult, op1=ALU.add)
        def tau_(e):
            tp = bank("tp", 6)
            nc.tensor.transpose(tp[:, 0:P], tz[:], ident[:])
            nc.scalar.copy(out=ntau[:], in_=tp[:, 0:4])

        def interleave(e, x, g, c0, c1, dst):
            if NB4:
                copy(e, dst[:].rearrange("p (c i) j -> p c j i", i=4),
                     raw[x, g][:, :, c0:c1].rearrange("p j (c i) -> p c j i", i=4))
            else:
                copy(e, dst[:], raw[x, g][:, :, c0:c1].rearrange("p j c -> p c j"))

        def quant(x, g, c0, c1, src):
            nc.vector.quantize_mx(
                out=sb("%sc%d" % (x, g), [P, D], U32)[:, c0:c1].bitcast(FP8X4),
                scales=sb("%ss%d" % (x, g), [P, D], U8)[:, c0:c1],
                in_=src[:].rearrange("p c j -> p (c j)"))

        def ck(e, g, h):
            interleave(e, "k", g, 256 * h, 256 * h + 256, sb("kg%d%d" % (g, h), [P, 256, 4], BF16))

        def zk(e, g, h):
            quant("k", g, 256 * h, 256 * h + 256, tiles["kg%d%d" % (g, h)])

        def cq(e, g, h):
            interleave(e, "q", g, P * h, P * h + P, sb("qg%d%d" % (g, h), [P, P, 4], BF16))

        def zq(e, g, h):
            quant("q", g, P * h, P * h + P, tiles["qg%d%d" % (g, h)])

        def S(e, g, t):
            mx(bank("s%d" % t, t)[:], tiles["qc%d" % g], tiles["qs%d" % g], slice(P * t, P * t + P),
               tiles["kc%d" % g], tiles["ks%d" % g], slice(0, D), g == 0, g == 1)

        def tv(e, b):
            words = raw["v", b // 2][:, b % 2].rearrange("p r w -> p (r w)").bitcast(F32)
            vp = bank("vp%d" % b, (4, 5, 6, 4)[b])
            for u in range(2):
                for r in range(2):
                    nc.tensor.transpose(vp[:, P * (2 * u + r):P * (2 * u + r) + P], words[:, 256 * r + u:256 * (r + 1):2], ident[:])

        def cv(e, b):
            vg = sb("vg%d" % b, [P, 256, 4], BF16)
            copy(e, vg[:].rearrange("p c j -> p (c j)").bitcast(F32).rearrange("p (t r u) -> p t r u", r=2, u=2),
                 tiles["vp%d" % b][:].rearrange("p (u r t) -> p t r u", u=2, r=2))

        def zv(e, b):
            nc.vector.quantize_mx(
                out=sb("vc%d" % b, [P, 256], U32)[:].bitcast(FP8X4),
                scales=sb("vs%d" % b, [P, 256], U8)[:],
                in_=tiles["vg%d" % b][:].rearrange("p c j -> p (c j)"))

        def ts(e, t):
            nc.vector.tensor_scalar(
                out=sb("lneg%d" % t, [P, 4, P], F32)[:], in0=tiles["s%d" % t][:].rearrange("p (m t) -> p t m", t=4),
                scalar1=ntau[:, t:t + 1], scalar2=None, op0=ALU.mult, op1=ALU.min,
                accum_out=sb("mn%d" % t, [P, 1], F32)[:])

        def ex(e, t):
            nc.scalar.activation(
                out=sb("e%d" % t, [P, 4, P], F32)[:], in_=tiles["lneg%d" % t][:], func=ACT.Exp,
                bias=tiles["mn%d" % t][:], scale=-1.0, accum_out=sb("sum%d" % t, [P, 1], F32)[:])

        def rc(e, t):
            nc.vector.reciprocal(out=sb("rs%d" % t, [P, 1], F32)[:], in_=tiles["sum%d" % t][:])

        def no(e, t):
            out, in_, rs = sb("c0%d" % t, [P, 4, P], F32), tiles["e%d" % t], tiles["rs%d" % t]
            if e == "A":
                nc.scalar.activation(out=out[:], in_=in_[:], func=ACT.Identity, bias=-1.0 / 512.0, scale=rs[:])
            else:
                eng = nc.vector if e == "D" else nc.gpsimd
                eng.tensor_scalar(out=out[:], in0=in_[:], scalar1=rs[:], scalar2=-1.0 / 512.0, op0=ALU.mult, op1=ALU.add)

        def trc(e, t):
            ct = bank("ct%d" % t, t)
            for u in range(4):
                nc.tensor.transpose(ct[:, P * u:P * u + P], tiles["c0%d" % t][:, u, :], ident[:])

        def tt(e, t):
            nc.vector.tensor_tensor(
                out=sb("cg%d" % t, [P, 4, 32, 4], BF16)[:],
                in0=tiles["ct%d" % t][:].rearrange("p (u m t) -> p t m u", u=4, t=4),
                in1=gain4[:].unsqueeze(1).unsqueeze(1).to_broadcast([P, 4, 32, 4]), op=ALU.mult)

        def zc(e, t):
            nc.vector.quantize_mx(
                out=cc[:, P * t:P * t + P].bitcast(FP8X4), scales=cs[:, P * t:P * t + P],
                in_=tiles["cg%d" % t][:].rearrange("p t m j -> p (t m j)"))

        def sh(e, h):
            for src, dst, w in ((cc, dc, 32), (cs, ds, 8)):
                nc.vector.tensor_copy(
                    out=dst[:].bitcast(I32).rearrange("p (t b m) -> p t b m", t=4, b=4)[:, :, 2 * h:2 * h + 2, :],
                    in_=src[:].bitcast(I32).rearrange("p (b t m) -> p t b m", t=4, b=4)[:, :, 2 * h:2 * h + 2, :])

        def shA(e):
            sh(e, 0)

        def shB(e):
            sh(e, 1)

        def A(e, h, m):
            pa = bank("a%d%d" % (h, m), (5, 6, 7, 4)[m])
            for r in range(2):
                mx(pa[:, 256 * r:256 * r + 256], tiles["vc%d" % m], tiles["vs%d" % m], slice(P * r, P * r + P),
                   cc, cs, slice(256 * h, 256 * h + 256), True, True)

        def ca(e, h, m):
            copy(e, sb("o%d%d" % (h, m), [P, 2, 256], F32)[:].rearrange("q n (b m t) -> q (n b) m t", b=2, t=4),
                 tiles["a%d%d" % (h, m)][:].rearrange("q (c t m) -> q c m t", c=4, t=4))

        def st(e, h, m):
            nc.sync.dma_start(
                out=out_0[0, 256 * m:256 * m + 256, 256 * h:256 * h + 256].rearrange("(n q) i -> q n i", n=2),
                in_=tiles["o%d%d" % (h, m)][:])

        def B(e, n):
            pb = bank("b%d" % n, (0, 1, 2, 3, 5, 6, 7, 4)[n])
            for t in range(4):
                mx(pb[:, P * t:P * t + P], dc, ds, slice(P * t, P * t + P),
                   tiles["vc%d" % (n // 2)], tiles["vs%d" % (n // 2)], slice(P * (n % 2), P * (n % 2) + P), True, True)

        def cb(e, n):
            copy(e, sb("og%d" % (n // 2), [P, 256, 4], BF16)[:, P * (n % 2):P * (n % 2) + P, :],
                 tiles["b%d" % n][:].rearrange("p (t m) -> p m t", t=4))

        def zw(e, w):
            nc.vector.quantize_mx(
                out=sb("wc%d" % w, [P, 256], U32)[:].bitcast(FP8X4),
                scales=sb("ws", [P, 1024], U8)[:, 256 * w:256 * w + 256],
                in_=tiles["og%d" % w][:].rearrange("p c j -> p (c j)"))

        words_out = out_1[0].rearrange("p m t -> p (m t)").bitcast(I32)
        scales_out = out_2[0].bitcast(I32)

        def sw(e, w):
            nc.sync.dma_start(out=words_out[:, 256 * w:256 * w + 256], in_=tiles["wc%d" % w][:].bitcast(I32))

        def dm(e, n):
            mx(bank("dm", 7)[:], tiles["kc0"], tiles["ks0"], slice(0, P), tiles["kc0"], tiles["ks0"], slice(0, D), True, True)

        steps = dict(dm=dm, ck=ck, zk=zk, cq=cq, zq=zq, S=S, tv=tv, cv=cv, zv=zv, ts=ts, ex=ex, rc=rc, no=no, tc=trc, tt=tt, zc=zc,
                     tau=tau_, A=A, ca=ca, st=st, B=B, cb=cb, shA=shA, shB=shB, zw=zw, sw=sw)
        for item in ORDER:
            f, e, ids = item.split(" ")
            steps[f](e, *[int(i) for i in ids])
        for r in range(4):
            eng = nc.sync if r % 2 else nc.scalar
            eng.dma_start(out=scales_out[4 * r:4 * r + 4, :], in_=tiles["ws"][32 * r:32 * r + 4, :].bitcast(I32))
